import numpy as np
import ml_dtypes


def mxq(x, axis, fmt="e4m3"):
    dtype, down = {"e4m3": (ml_dtypes.float8_e4m3fn, 7), "e5m2": (ml_dtypes.float8_e5m2, 14)}[fmt]
    v = np.moveaxis(np.asarray(x, np.float32).astype(ml_dtypes.bfloat16).astype(np.float64), axis, -1)
    blocks = v.reshape(v.shape[:-1] + (-1, 32))
    amax = np.abs(blocks).max(-1, keepdims=True)
    byte = np.maximum(np.where(amax > 0, np.frexp(amax)[1] - 1 + 127, 0) - down, 1)
    scale = np.exp2(byte - 127.0)
    codes = (blocks / scale).astype(np.float32).astype(dtype).astype(np.float64)
    return np.moveaxis((codes * scale).reshape(v.shape), -1, axis)


WIDE = False


def mx_kscale(k):
    if not WIDE:
        return np.ones(k)
    levels = np.array([10, -10, 5, -5, 0])
    if k % 512:
        return np.exp2(np.random.permutation(np.resize(levels, k // 32))).repeat(32)
    a = np.empty((k // 512, 16))
    for p in range(k // 512):
        a[p, :8] = np.random.permutation(np.resize(levels, 8))
        for g in range(8):
            far = levels[np.abs(levels - a[p, g]) >= 10]
            a[p, g + 8] = far[np.random.randint(len(far))]
    return np.exp2(a.ravel()).repeat(32)


def f64(x):
    return np.asarray(x).astype(np.float64)


def striped(idx):
    return np.tile(idx.reshape(-1, 16).T, (8, 1)).astype(np.uint16)


def unstriped(offs):
    return offs[:16].T.reshape(-1).astype(np.int64)


E2M1 = np.array([0.0, 0.5, 1.0, 1.5, 2.0, 3.0, 4.0, 6.0, -0.0, -0.5, -1.0, -1.5, -2.0, -3.0, -4.0, -6.0])


def pack_weight(w, fmt):
    k, n = w.shape
    w = f64(np.asarray(w, np.float32).astype(ml_dtypes.bfloat16)).reshape(k // 32, 32, n)
    amax = np.abs(w).max(1)
    if fmt == "e4m3":
        byte = np.frexp(amax)[1] - 1 + 127 - 7
    else:
        mant, ex = np.frexp(amax / 6.0)
        byte = np.where(mant > 0.5, ex, ex - 1) + 127
    byte = np.clip(np.where(amax > 0, byte, 1), 1, 254)
    scaled = (w * np.exp2(127.0 - byte)[:, None, :]).reshape(k, n).astype(np.float32)
    by_word = np.ascontiguousarray(scaled.reshape(k // 512, 128, 4, n).transpose(0, 1, 3, 2))
    if fmt == "e4m3":
        words = by_word.astype(ml_dtypes.float8_e4m3fn).view(np.uint8)
    else:
        c = by_word.astype(ml_dtypes.float4_e2m1fn).view(np.uint8) & 0xF
        words = (c[..., 0::2] | (c[..., 1::2] << 4)).reshape(k // 512, 128, 2 * n)
    return np.ascontiguousarray(words), np.ascontiguousarray(byte.astype(np.uint8).reshape(k // 512, 16, n))


def unpack_weight(words, scales, fmt):
    g, _, n = scales.shape
    words = np.ascontiguousarray(words).reshape(g, 128, n, -1)
    if fmt == "e4m3":
        vals = words.view(ml_dtypes.float8_e4m3fn).astype(np.float64)
    else:
        nib = np.empty((g, 128, n, 4), np.uint8)
        nib[..., 0::2] = words & 0xF
        nib[..., 1::2] = words >> 4
        vals = E2M1[nib]
    vals = vals * np.repeat(np.exp2(scales.astype(np.float64) - 127.0), 8, axis=1)[..., None]
    return vals.transpose(0, 1, 3, 2).reshape(g * 512, n)


def relu(v):
    return np.maximum(v, 0.0)


K, T, E, C, H, N = 512, 1536, 8, 128, 512, 512


def by_expert(wq, xq):
    return np.concatenate([wq[e].T @ xq[:, e * C:(e + 1) * C] for e in range(E)], axis=1)


def setup_inputs():
    n = np.random.standard_normal
    s = mx_kscale(K)[:, None]
    u = mx_kscale(H)
    x = pack_weight(n((K, T)) * s, "e4m3")
    return {
        "x_words": x[0],
        "x_scales": x[1],
        "xr": n((N, T)).astype(np.float32),
        "w1": (n((E, K, H)) / np.sqrt(K) / s[None] * u[None, None, :]).astype(np.float32),
        "w2": (n((E, H, N)) / np.sqrt(H) / u[None, :, None]).astype(np.float32),
        "gate": np.tile(np.random.uniform(0.2, 1.0, E * C), (N, 1)).astype(np.float32),
        "offs": striped(np.random.permutation(T)[:E * C]),
    }


def reference(x_words, x_scales, xr, w1, w2, gate, offs):
    idx = unstriped(offs)
    xq = unpack_weight(x_words, x_scales, "e4m3")[:, idx]
    h = relu(by_expert(mxq(f64(w1), 1, "e4m3"), xq))
    y = by_expert(mxq(f64(w2), 1, "e4m3"), mxq(h, 0, "e4m3"))
    out = f64(xr).copy()
    out[:, idx] += f64(gate) * y
    return out

@@ -1,0 +1,256 @@
+from contextlib import ExitStack
+
+import concourse.mybir as mybir
+
+K, T, E, C, H, N = 512, 1536, 8, 128, 512, 512
+S = E * C
+FLOPS = 2 * S * (K * H + H * N)
+
+F32 = mybir.dt.float32
+BF16 = mybir.dt.bfloat16
+I32 = mybir.dt.int32
+U32 = mybir.dt.uint32
+U16 = mybir.dt.uint16
+U8 = mybir.dt.uint8
+FP8X4 = mybir.dt.float8_e4m3fn_x4
+MULT = mybir.AluOpType.mult
+ADD = mybir.AluOpType.add
+RELU = mybir.ActivationFunctionType.Relu
+
+P = 128
+PACK = 4
+HALF = N // 2
+PAIR = 2 * C
+
+LOADS = "a1 a0 b00 g0 b11 b01 a2 b10 a3 b2 b3 g1 b4 a4 b5 a5 a7 a6 b6 b7".split()
+STEPS = "a00v a10 b10v a11v a01 r0 r1 b00v b01v a21 s b11 a20 y01 a30 y00 a31v r2 b21 r3 b30 b20 a51v y02 b31v a40v y03 a41 a50 y11 b41 y10 y12 b40 r4 x b50 y13 r5 b51v a70 a60 a61 y21 y20 a71v b60 y22 y23 r6 b70 b61 r7 b71 y31 y33 y30 y32".split()
+PINS = {"y01":"a2","y02":"a3","y03":"b2","y10":"a4","y11":"b3","y12":"a5","r4":"a5","y13":"b4","r5":"b4","y20":"a6","r7":"a7","Gb21":"a5","Gb11":"a2","Gb31":"a7","Gb10":"a3","y31":"b6","Ga2":"b00","y30":"b6","Ga6":"b5","y00":"b11","s":"a0","r6":"a7","y23":"a7","y32":"b7"}
+BY_HALF = [0,2,3]
+ADD_ON_GPSIMD = []
+T_SPLIT = True
+RING = 4
+Y_BUFS = 3
+REST_AFTER = "a0"
+LAST_CUTS = 2
+
+
+def tile_moe_res_mlp_relu_kernel(tc, x_words, x_scales, xr, w1, w2, gate, offs, out):
+    nc = tc.nc
+
+    with ExitStack() as ctx:
+        keep = ctx.enter_context(tc.tile_pool(name="keep", bufs=1))
+        arena = ctx.enter_context(tc.tile_pool(name="arena", bufs=1))
+        work = ctx.enter_context(tc.tile_pool(name="work", bufs=3))
+        psum = ctx.enter_context(tc.psum_pool(name="psum", bufs=4))
+
+        offsets = keep.tile([P, S // 16], U16, name="offsets")
+        token_words = keep.tile([P, T], I32, name="token_words")
+        token_scales = keep.tile([P, T], U8, name="token_scales")
+        slot_words = keep.tile([P, S], U32, name="slot_words", align_bytes=64)
+        first_scales = keep.tile([P, PAIR], U8, name="first_scales", align_bytes=64)
+        h_codes = keep.tile([P, S], U32, name="h_codes", align_bytes=64)
+        h_scales = keep.tile([P, S], U8, name="h_scales", align_bytes=64)
+        gates = keep.tile([P, S], F32, name="gates")
+        routed = [keep.tile([P, T], F32, name="routed%d" % b) for b in range(4)]
+        result = {}
+
+        nc.sync.dma_start(offsets[:], offs)
+        nc.sync.dma_start(token_words[:], x_words[0].rearrange("p t r -> p (t r)").bitcast(I32))
+        for q in range(4):
+            nc.sync.dma_start(
+                token_scales[32 * q : 32 * q + 32, :].bitcast(I32),
+                x_scales[0, 4 * q : 4 * q + 4, :].bitcast(I32).partition_broadcast(8),
+            )
+        for b in range(4):
+            nc.vector.memset(routed[b][:], 0.0)
+
+        free = {}
+        ends = {}
+        reads = {}
+        used = [0]
+
+        def arena_tile(key, shape, size):
+            tile = arena.tile(shape, F32, name="raw_" + key, align_bytes=64, offset=used[0])
+            free[key] = used[0]
+            used[0] += size
+            ends[key] = used[0]
+            reads[key] = size // 4096
+            return tile
+
+        def staged(step, shape, dtype, size, name, bufs):
+            if step in PINS:
+                place = free[PINS[step]]
+                free[PINS[step]] += size
+                assert free[PINS[step]] <= ends[PINS[step]] and reads[PINS[step]] == 0
+                return arena.tile(shape, dtype, name=name + "_" + step, align_bytes=64, offset=place)
+            return work.tile(shape, dtype, name=name, align_bytes=64, bufs=bufs)
+
+        w1_raw = {}
+        w2_raw = {}
+        for load in LOADS:
+            kind, e = load[0], int(load[1])
+            if kind == "a":
+                tile = arena_tile(load, [P, PACK, H], 8192)
+                nc.sync.dma_start(tile[:], w1[e].rearrange("(p j) c -> p j c", j=PACK))
+                w1_raw[e] = tile
+            elif kind == "b" and len(load) == 2:
+                tile = arena_tile(load, [P, PACK, N], 8192)
+                nc.sync.dma_start(tile[:], w2[e].rearrange("(p j) c -> p j c", j=PACK))
+                for half in range(2):
+                    w2_raw[e, half] = tile[:, :, half * HALF : (half + 1) * HALF]
+            elif kind == "b":
+                half = int(load[2])
+                tile = arena_tile(load, [P, PACK, HALF], 4096)
+                nc.sync.dma_start(
+                    tile[:], w2[e].rearrange("(p j) c -> p j c", j=PACK)[:, :, half * HALF : (half + 1) * HALF]
+                )
+                w2_raw[e, half] = tile[:]
+            else:
+                cols = slice(0, PAIR) if e == 0 else slice(PAIR, S)
+                nc.sync.dma_start(gates[:, cols], gate[:P, cols])
+
+        nc.vector.tensor_copy(slot_words[:], token_words[:].bitcast(U32).indirect(offsets[:]))
+        nc.vector.tensor_copy(first_scales[:], token_scales[:].indirect(offsets[:, :16]))
+        slot_scales = {0: first_scales[:, :C], 1: first_scales[:, C:]}
+
+        grouped = {}
+        filled = {}
+        acc1 = {}
+        acc2 = {}
+        w2_q = {}
+        relu_done = set()
+        multiplied = set()
+        scattered = [0] * 4
+
+        def group_tile(key):
+            if key not in grouped:
+                grouped[key] = staged(key, [P, 4 * H], BF16, 4096, "grouped", RING)
+                filled[key] = 0
+            filled[key] += 1
+            return grouped[key]
+
+        def copy(on_vector, dst, src):
+            if on_vector:
+                nc.vector.tensor_copy(out=dst, in_=src)
+            else:
+                nc.scalar.copy(out=dst, in_=src)
+
+        def quantise(key):
+            codes = work.tile([P, H], U32, name="codes_" + key[1], align_bytes=64)
+            scales = work.tile([P, H], U8, name="scales_" + key[1], align_bytes=64)
+            nc.vector.quantize_mx(codes[:].bitcast(FP8X4), scales[:], grouped[key][:])
+            return codes, scales
+
+        def mx(acc, lhs, lhs_scales, rhs, rhs_scales):
+            nc.tensor.matmul_mx(
+                out=acc,
+                lhsT=lhs.bitcast(FP8X4),
+                lhsT_scale=lhs_scales,
+                rhs=rhs.bitcast(FP8X4),
+                rhs_scale=rhs_scales,
+                start=True,
+                stop=True,
+            )
+
+        def second_products():
+            for e, half in list(w2_q):
+                if e in relu_done and (e, half) not in multiplied:
+                    multiplied.add((e, half))
+                    pair, u = divmod(e, 2)
+                    if (pair, half) not in acc2:
+                        acc2[pair, half] = psum.tile([P, 2, PAIR], F32, name="acc2")
+                    codes, scales = w2_q[e, half]
+                    slots = slice(e * C, (e + 1) * C)
+                    for v in range(2):
+                        cols = slice(v * P, (v + 1) * P)
+                        mx(
+                            acc2[pair, half][:, v, u * C : (u + 1) * C],
+                            codes[:, cols],
+                            scales[:, cols],
+                            h_codes[:, slots],
+                            h_scales[:, slots],
+                        )
+
+        for step in STEPS:
+            kind = step[0]
+            on_vector = step[-1] == "v"
+            if kind == "a":
+                e, half = int(step[1]), int(step[2])
+                key = "Ga%d" % e
+                tile = group_tile(key)
+                src = w1_raw[e][:].rearrange("p j (m t) -> p m j t", t=PACK)
+                dst = tile[:].rearrange("p (t m j) -> p m j t", t=PACK, j=PACK)
+                if T_SPLIT:
+                    ts = slice(half * 2, half * 2 + 2)
+                    copy(on_vector, dst[:, :, :, ts], src[:, :, :, ts])
+                else:
+                    ms = slice(half * 64, (half + 1) * 64)
+                    copy(on_vector, dst[:, ms], src[:, ms])
+                reads["a%d" % e] -= 1
+                if filled[key] == 2:
+                    codes, scales = quantise(key)
+                    acc = psum.tile([P, PACK, C], F32, name="acc1")
+                    slots = slice(e * C, (e + 1) * C)
+                    for t in range(PACK):
+                        cols = slice(t * P, (t + 1) * P)
+                        mx(acc[:, t, :], codes[:, cols], scales[:, cols], slot_words[:, slots], slot_scales[e])
+                    acc1[e] = acc
+            elif kind == "x":
+                for b in range(4):
+                    assert reads["a%d" % b] == 0
+                    free["a%d" % b] = ends["a%d" % b]
+                    result[b] = arena.tile([P, T], F32, name="result%d" % b, align_bytes=64, offset=ends["a%d" % b] - 8192)
+                    nc.sync.dma_start(result[b][:], xr[b * P : (b + 1) * P, :])
+            elif kind == "s":
+                rest = staged(step, [P, S - PAIR], U8, 1024, "rest_scales", 1)
+                nc.vector.tensor_copy(rest[:], token_scales[:].indirect(offsets[:, 16:]))
+                for later in range(2, E):
+                    slot_scales[later] = rest[:, (later - 2) * C : (later - 1) * C]
+            elif kind == "r":
+                e = int(step[1])
+                hidden = staged(step, [P, C, PACK], BF16, 1024, "hidden", 3)
+                nc.scalar.activation(hidden[:], acc1[e][:].rearrange("p t c -> p c t"), RELU)
+                slots = slice(e * C, (e + 1) * C)
+                nc.vector.quantize_mx(
+                    h_codes[:, slots].bitcast(FP8X4), h_scales[:, slots], hidden[:].rearrange("p c t -> p (c t)")
+                )
+                relu_done.add(e)
+                second_products()
+            elif kind == "b":
+                e, half = int(step[1]), int(step[2])
+                pair, u = divmod(e, 2)
+                by_half = pair in BY_HALF
+                key = "Gb%d%d" % (pair, half if by_half else u)
+                part = u if by_half else half
+                tile = group_tile(key)
+                dst = tile[:, part * 4 * HALF : (part + 1) * 4 * HALF].rearrange("p (c i j) -> p c j i", i=4, j=PACK)
+                copy(on_vector, dst, w2_raw[e, half].rearrange("p j (c i) -> p c j i", i=4))
+                reads["b%d" % e if "b%d" % e in reads else "b%d%d" % (e, half)] -= 1
+                if filled[key] == 2:
+                    codes, scales = quantise(key)
+                    for other in range(2):
+                        cols = slice(other * HALF, (other + 1) * HALF)
+                        owner = (2 * pair + other, half) if by_half else (e, other)
+                        w2_q[owner] = codes[:, cols], scales[:, cols]
+                    second_products()
+            else:
+                pair, b = int(step[1]), int(step[2])
+                assert (2 * pair, b // 2) in multiplied and (2 * pair + 1, b // 2) in multiplied
+                y = staged(step, [P, PAIR], F32, 1024, "y", Y_BUFS)
+                window = routed[b][:].indirect(offsets[:, pair * 16 : (pair + 1) * 16])
+                sums = acc2[pair, b // 2][:, b % 2, :]
+                weights = gates[:, pair * PAIR : (pair + 1) * PAIR]
+                if kind == "y":
+                    nc.scalar.copy(out=y[:], in_=sums)
+                    nc.vector.tensor_tensor(window, y[:], weights, MULT)
+                else:
+                    nc.vector.tensor_tensor(y[:], sums, weights, MULT)
+                    nc.vector.tensor_copy(window, y[:])
+                scattered[b] += 1
+                if scattered[b] == 4:
+                    engine = nc.gpsimd if b in ADD_ON_GPSIMD else nc.vector
+                    cuts = LAST_CUTS if min(scattered) == 4 else 1
+                    for cut in range(cuts):
+                        cols = slice(cut * T // cuts, (cut + 1) * T // cuts)
+                        engine.tensor_tensor(result[b][:, cols], result[b][:, cols], routed[b][:, cols], ADD)
+                        nc.sync.dma_start(out[b * P : (b + 1) * P, cols], result[b][:, cols])

@@ -22,14 +22,14 @@ PACK = 4
 HALF = N // 2
 PAIR = 2 * C
 
-LOADS = "a1 a0 b00 g0 b11 b01 a2 b10 a3 b2 b3 g1 b4 a4 b5 a5 a7 a6 b6 b7".split()
-STEPS = "a00v a10 b10v a11v a01 r0 r1 b00v b01v a21 s b11 a20 y01 a30 y00 a31v r2 b21 r3 b30 b20 a51v y02 b31v a40v y03 a41 a50 y11 b41 y10 y12 b40 r4 x b50 y13 r5 b51v a70 a60 a61 y21 y20 a71v b60 y22 y23 r6 b70 b61 r7 b71 y31 y33 y30 y32".split()
-PINS = {"y01":"a2","y02":"a3","y03":"b2","y10":"a4","y11":"b3","y12":"a5","r4":"a5","y13":"b4","r5":"b4","y20":"a6","r7":"a7","Gb21":"a5","Gb11":"a2","Gb31":"a7","Gb10":"a3","y31":"b6","Ga2":"b00","y30":"b6","Ga6":"b5","y00":"b11","s":"a0","r6":"a7","y23":"a7","y32":"b7"}
+LOADS = "a1 g0 a0 b00 b01 b10 b11 a2 b2 a3 b3 a5 a4 g1 b5 b4 a6 a7 b7 b6".split()
+STEPS = "a11v a01 a00 b10v a10 r0 a21 s b00v r1 y00 a31 y01 a20 b01 b31 a30 a41 r2 b11 a51v b21v b30 y02 a40v r3 b20v y03 a50 y10 b51v y12 r5 x a71v b50 b61 b70 b60 b41 y11 b40 r4 a60 y13 a70 y23 a61 b71 y21 r6 y22 r7 y33 y20 y32 y30 y31".split()
+PINS = {"s":"a1","r2":"a3","y13":"b4","y22":"a6","y23":"b6","y30":"b7","r3":"b3","y10":"a3","Ga2":"a0","r6":"b7","Ga4":"b01","y33":"b6","Gb10":"a2","y31":"b7","y32":"b7","r1":"a0","y21":"a6","y12":"a4","Gb30":"b5","y20":"a6"}
 BY_HALF = [0,2,3]
 ADD_ON_GPSIMD = []
 T_SPLIT = True
-RING = 4
-Y_BUFS = 3
+RING = 6
+Y_BUFS = 5
 REST_AFTER = "a0"
 LAST_CUTS = 2
 
@@ -62,7 +62,7 @@ def tile_moe_res_mlp_relu_kernel(tc, x_words, x_scales, xr, w1, w2, gate, offs, 
                 x_scales[0, 4 * q : 4 * q + 4, :].bitcast(I32).partition_broadcast(8),
             )
         for b in range(4):
-            nc.vector.memset(routed[b][:], 0.0)
+            nc.gpsimd.memset(routed[b][:], 0.0)
 
         free = {}
         ends = {}
@@ -223,8 +223,22 @@ def tile_moe_res_mlp_relu_kernel(tc, x_words, x_scales, xr, w1, w2, gate, offs, 
                 key = "Gb%d%d" % (pair, half if by_half else u)
                 part = u if by_half else half
                 tile = group_tile(key)
-                dst = tile[:, part * 4 * HALF : (part + 1) * 4 * HALF].rearrange("p (c i j) -> p c j i", i=4, j=PACK)
-                copy(on_vector, dst, w2_raw[e, half].rearrange("p j (c i) -> p c j i", i=4))
+                dst = tile[:, part * 4 * HALF : (part + 1) * 4 * HALF]
+                if step[-1] == "g":
+                    nc.gpsimd.tensor_scalar(
+                        dst.rearrange("p (c j) -> p c j", j=PACK),
+                        w2_raw[e, half].rearrange("p j c -> p c j"),
+                        1.0,
+                        0.0,
+                        MULT,
+                        ADD,
+                    )
+                else:
+                    copy(
+                        on_vector,
+                        dst.rearrange("p (c i j) -> p c j i", i=4, j=PACK),
+                        w2_raw[e, half].rearrange("p j (c i) -> p c j i", i=4),
+                    )
                 reads["b%d" % e if "b%d" % e in reads else "b%d%d" % (e, half)] -= 1
                 if filled[key] == 2:
                     codes, scales = quantise(key)

@@ -1,6 +1,7 @@
 from contextlib import ExitStack
 
 import concourse.mybir as mybir
+from concourse.masks import make_identity
 
 K, T, E, C, H, N = 512, 1536, 8, 128, 512, 512
 S = E * C
@@ -22,16 +23,14 @@ PACK = 4
 HALF = N // 2
 PAIR = 2 * C
 
-LOADS = "a1 g0 a0 b00 b01 b10 b11 a2 b2 a3 b3 a5 a4 g1 b5 b4 a6 a7 b7 b6".split()
-STEPS = "a11v a01 a00 b10v a10 r0 a21 s b00v r1 y00 a31 y01 a20 b01 b31 a30 a41 r2 b11 a51v b21v b30 y02 a40v r3 b20v y03 a50 y10 b51v y12 r5 x a71v b50 b61 b70 b60 b41 y11 b40 r4 a60 y13 a70 y23 a61 b71 y21 r6 y22 r7 y33 y20 y32 y30 y31".split()
-PINS = {"s":"a1","r2":"a3","y13":"b4","y22":"a6","y23":"b6","y30":"b7","r3":"b3","y10":"a3","Ga2":"a0","r6":"b7","Ga4":"b01","y33":"b6","Gb10":"a2","y31":"b7","y32":"b7","r1":"a0","y21":"a6","y12":"a4","Gb30":"b5","y20":"a6"}
-BY_HALF = [0,2,3]
-ADD_ON_GPSIMD = []
+LOADS = "g0 a0 b00 b01 a1 a2 b10 b11 a3 a4 b3 b2 a5 b5 a6 b4 g1 b6 a7 b7".split()
+STEPS = "a01v a00 b00 s a11v b11v a10 a21v r0 b01 r1 b10 a30 a20v y03 y01 y02 a41 r2 b21 b30 y00 a40 a50v a31v r3 b50 b20 a61v b31v y11 y12 a51 r5 y10 b40 b41 a60 b61 y13 a70 b51v b71 r4 y21 r6 b70 a71 y23 r7 b60 y20 x y31 y30 y33 p10 p11 p01 p00 y32 e0 o11 p30 o00 o30 y22 o10 e3 e1 o01 e2".split()
+X_ORDER = [1,3,2,0]
+RAW = 14
+BY_HALF = [0,1,3]
 T_SPLIT = True
-RING = 6
-Y_BUFS = 5
-REST_AFTER = "a0"
-LAST_CUTS = 2
+RING = 10
+LAST_CUTS = 4
 
 
 def tile_moe_res_mlp_relu_kernel(tc, x_words, x_scales, xr, w1, w2, gate, offs, out):
@@ -64,26 +63,16 @@ def tile_moe_res_mlp_relu_kernel(tc, x_words, x_scales, xr, w1, w2, gate, offs, 
         for b in range(4):
             nc.gpsimd.memset(routed[b][:], 0.0)
 
-        free = {}
-        ends = {}
-        reads = {}
-        used = [0]
+        on_pe = [sum(1 for step in STEPS if step[:2] == "p%d" % b) for b in range(4)]
+        if max(on_pe):
+            identity = keep.tile([P, P], F32, name="identity")
+            make_identity(nc, identity[:])
 
         def arena_tile(key, shape, size):
-            tile = arena.tile(shape, F32, name="raw_" + key, align_bytes=64, offset=used[0])
-            free[key] = used[0]
-            used[0] += size
-            ends[key] = used[0]
-            reads[key] = size // 4096
-            return tile
+            return arena.tile(shape, F32, name="raw", bufs=RAW)
 
-        def staged(step, shape, dtype, size, name, bufs):
-            if step in PINS:
-                place = free[PINS[step]]
-                free[PINS[step]] += size
-                assert free[PINS[step]] <= ends[PINS[step]] and reads[PINS[step]] == 0
-                return arena.tile(shape, dtype, name=name + "_" + step, align_bytes=64, offset=place)
-            return work.tile(shape, dtype, name=name, align_bytes=64, bufs=bufs)
+        def staged(shape, dtype):
+            return work.tile(shape, dtype, name="stage", align_bytes=64, bufs=RING)
 
         w1_raw = {}
         w2_raw = {}
@@ -114,6 +103,7 @@ def tile_moe_res_mlp_relu_kernel(tc, x_words, x_scales, xr, w1, w2, gate, offs, 
         slot_scales = {0: first_scales[:, :C], 1: first_scales[:, C:]}
 
         grouped = {}
+        turned = {}
         filled = {}
         acc1 = {}
         acc2 = {}
@@ -124,7 +114,7 @@ def tile_moe_res_mlp_relu_kernel(tc, x_words, x_scales, xr, w1, w2, gate, offs, 
 
         def group_tile(key):
             if key not in grouped:
-                grouped[key] = staged(key, [P, 4 * H], BF16, 4096, "grouped", RING)
+                grouped[key] = staged([P, 4 * H], BF16)
                 filled[key] = 0
             filled[key] += 1
             return grouped[key]
@@ -186,7 +176,6 @@ def tile_moe_res_mlp_relu_kernel(tc, x_words, x_scales, xr, w1, w2, gate, offs, 
                 else:
                     ms = slice(half * 64, (half + 1) * 64)
                     copy(on_vector, dst[:, ms], src[:, ms])
-                reads["a%d" % e] -= 1
                 if filled[key] == 2:
                     codes, scales = quantise(key)
                     acc = psum.tile([P, PACK, C], F32, name="acc1")
@@ -196,19 +185,46 @@ def tile_moe_res_mlp_relu_kernel(tc, x_words, x_scales, xr, w1, w2, gate, offs, 
                         mx(acc[:, t, :], codes[:, cols], scales[:, cols], slot_words[:, slots], slot_scales[e])
                     acc1[e] = acc
             elif kind == "x":
-                for b in range(4):
-                    assert reads["a%d" % b] == 0
-                    free["a%d" % b] = ends["a%d" % b]
-                    result[b] = arena.tile([P, T], F32, name="result%d" % b, align_bytes=64, offset=ends["a%d" % b] - 8192)
+                for b in X_ORDER:
+                    result[b] = arena_tile("x", [P, T], 6144)
                     nc.sync.dma_start(result[b][:], xr[b * P : (b + 1) * P, :])
+            elif kind == "p":
+                b, chunk = int(step[1]), int(step[2])
+                assert scattered[b] == 4 and chunk < on_pe[b]
+                summed = psum.tile([P, 4, P], F32, name="acc1")
+                for i in range(4):
+                    part = slice(chunk * 512 + i * P, chunk * 512 + (i + 1) * P)
+                    for first, source in ((True, result[b]), (False, routed[b])):
+                        nc.tensor.matmul(
+                            summed[:, i, :], source[:, part], identity[:], start=first, stop=not first, is_transpose=True
+                        )
+                turned[b, chunk] = staged([P, 4, P], F32)
+                nc.scalar.copy(out=turned[b, chunk][:], in_=summed[:])
+            elif kind == "o":
+                b, chunk = int(step[1]), int(step[2])
+                cols = slice(chunk * 512, (chunk + 1) * 512)
+                back = psum.tile([P, 4, P], F32, name="acc1")
+                for i in range(4):
+                    nc.tensor.transpose(back[:, i, :], turned[b, chunk][:, i, :], identity[:])
+                nc.scalar.copy(out=result[b][:, cols], in_=back[:].rearrange("p i t -> p (i t)"))
+                nc.sync.dma_start(out[b * P : (b + 1) * P, cols], result[b][:, cols])
+            elif kind == "e":
+                b = int(step[1])
+                assert scattered[b] == 4
+                start = on_pe[b] * 512
+                cuts = LAST_CUTS if step == [other for other in STEPS if other[0] == "e"][-1] else 1
+                for cut in range(cuts if start < T else 0):
+                    cols = slice(start + cut * (T - start) // cuts, start + (cut + 1) * (T - start) // cuts)
+                    nc.vector.tensor_tensor(result[b][:, cols], result[b][:, cols], routed[b][:, cols], ADD)
+                    nc.sync.dma_start(out[b * P : (b + 1) * P, cols], result[b][:, cols])
             elif kind == "s":
-                rest = staged(step, [P, S - PAIR], U8, 1024, "rest_scales", 1)
+                rest = staged([P, S - PAIR], U8)
                 nc.vector.tensor_copy(rest[:], token_scales[:].indirect(offsets[:, 16:]))
                 for later in range(2, E):
                     slot_scales[later] = rest[:, (later - 2) * C : (later - 1) * C]
             elif kind == "r":
                 e = int(step[1])
-                hidden = staged(step, [P, C, PACK], BF16, 1024, "hidden", 3)
+                hidden = staged([P, C, PACK], BF16)
                 nc.scalar.activation(hidden[:], acc1[e][:].rearrange("p t c -> p c t"), RELU)
                 slots = slice(e * C, (e + 1) * C)
                 nc.vector.quantize_mx(
@@ -239,7 +255,6 @@ def tile_moe_res_mlp_relu_kernel(tc, x_words, x_scales, xr, w1, w2, gate, offs, 
                         dst.rearrange("p (c i j) -> p c j i", i=4, j=PACK),
                         w2_raw[e, half].rearrange("p j (c i) -> p c j i", i=4),
                     )
-                reads["b%d" % e if "b%d" % e in reads else "b%d%d" % (e, half)] -= 1
                 if filled[key] == 2:
                     codes, scales = quantise(key)
                     for other in range(2):
@@ -250,7 +265,7 @@ def tile_moe_res_mlp_relu_kernel(tc, x_words, x_scales, xr, w1, w2, gate, offs, 
             else:
                 pair, b = int(step[1]), int(step[2])
                 assert (2 * pair, b // 2) in multiplied and (2 * pair + 1, b // 2) in multiplied
-                y = staged(step, [P, PAIR], F32, 1024, "y", Y_BUFS)
+                y = staged([P, PAIR], F32)
                 window = routed[b][:].indirect(offsets[:, pair * 16 : (pair + 1) * 16])
                 sums = acc2[pair, b // 2][:, b % 2, :]
                 weights = gates[:, pair * PAIR : (pair + 1) * PAIR]
@@ -261,10 +276,3 @@ def tile_moe_res_mlp_relu_kernel(tc, x_words, x_scales, xr, w1, w2, gate, offs, 
                     nc.vector.tensor_tensor(y[:], sums, weights, MULT)
                     nc.vector.tensor_copy(window, y[:])
                 scattered[b] += 1
-                if scattered[b] == 4:
-                    engine = nc.gpsimd if b in ADD_ON_GPSIMD else nc.vector
-                    cuts = LAST_CUTS if min(scattered) == 4 else 1
-                    for cut in range(cuts):
-                        cols = slice(cut * T // cuts, (cut + 1) * T // cuts)
-                        engine.tensor_tensor(result[b][:, cols], result[b][:, cols], routed[b][:, cols], ADD)
-                        nc.sync.dma_start(out[b * P : (b + 1) * P, cols], result[b][:, cols])

@@ -23,11 +23,11 @@ PACK = 4
 HALF = N // 2
 PAIR = 2 * C
 
-LOADS = "g0 a0 b00 b01 a1 a2 b10 b11 a3 a4 b3 b2 a5 b5 a6 b4 g1 b6 a7 b7".split()
-STEPS = "a01v a00 b00 s a11v b11v a10 a21v r0 b01 r1 b10 a30 a20v y03 y01 y02 a41 r2 b21 b30 y00 a40 a50v a31v r3 b50 b20 a61v b31v y11 y12 a51 r5 y10 b40 b41 a60 b61 y13 a70 b51v b71 r4 y21 r6 b70 a71 y23 r7 b60 y20 x y31 y30 y33 p10 p11 p01 p00 y32 e0 o11 p30 o00 o30 y22 o10 e3 e1 o01 e2".split()
-X_ORDER = [1,3,2,0]
+LOADS = "b10 a0 b00 g0 a1 b11 b01 a2 a3 b3 b2 a4 g1 a5 a6 b5 b4 a7 b7 b6".split()
+STEPS = "s b00 a01 b10 a00v a10 r0 a11v b11 r1 a21v y00 y01 a30 b01v a20 a31 y02 b20v b31 b30 r3 r2 a40 y03 a50v b21v a41 y11 b51v y12 a51 y10 a60 b50 r4 y13 r5 b71v b40 b41 x a71 a61 y21 a70 r6 y22 b70 y20 b60 r7 y23 y31 y30 b61 y32 p10 p01 p00 e0 e2 o10 y33 o01 e1 o00 e3".split()
+X_ORDER = [0,1,2,3]
 RAW = 14
-BY_HALF = [0,1,3]
+BY_HALF = [0,2,3]
 T_SPLIT = True
 RING = 10
 LAST_CUTS = 4

from contextlib import ExitStack

import concourse.mybir as mybir
from concourse.masks import make_identity

K, T, E, C, H, N = 512, 1536, 8, 128, 512, 512
S = E * C
FLOPS = 2 * S * (K * H + H * N)

F32 = mybir.dt.float32
BF16 = mybir.dt.bfloat16
I32 = mybir.dt.int32
U32 = mybir.dt.uint32
U16 = mybir.dt.uint16
U8 = mybir.dt.uint8
FP8X4 = mybir.dt.float8_e4m3fn_x4
MULT = mybir.AluOpType.mult
ADD = mybir.AluOpType.add
RELU = mybir.ActivationFunctionType.Relu

P = 128
PACK = 4
HALF = N // 2
PAIR = 2 * C

LOADS = "b10 a0 b00 g0 a1 b11 b01 a2 a3 b3 b2 a4 g1 a5 a6 b5 b4 a7 b7 b6".split()
STEPS = "s b00 a01 b10 a00v a10 r0 a11v b11 r1 a21v y00 y01 a30 b01v a20 a31 y02 b20v b31 b30 r3 r2 a40 y03 a50v b21v a41 y11 b51v y12 a51 y10 a60 b50 r4 y13 r5 b71v b40 b41 x a71 a61 y21 a70 r6 y22 b70 y20 b60 r7 y23 y31 y30 b61 y32 p10 p01 p00 e0 e2 o10 y33 o01 e1 o00 e3".split()
X_ORDER = [0,1,2,3]
RAW = 14
BY_HALF = [0,2,3]
T_SPLIT = True
RING = 10
LAST_CUTS = 4


def tile_moe_res_mlp_relu_kernel(tc, x_words, x_scales, xr, w1, w2, gate, offs, out):
    nc = tc.nc

    with ExitStack() as ctx:
        keep = ctx.enter_context(tc.tile_pool(name="keep", bufs=1))
        arena = ctx.enter_context(tc.tile_pool(name="arena", bufs=1))
        work = ctx.enter_context(tc.tile_pool(name="work", bufs=3))
        psum = ctx.enter_context(tc.psum_pool(name="psum", bufs=4))

        offsets = keep.tile([P, S // 16], U16, name="offsets")
        token_words = keep.tile([P, T], I32, name="token_words")
        token_scales = keep.tile([P, T], U8, name="token_scales")
        slot_words = keep.tile([P, S], U32, name="slot_words", align_bytes=64)
        first_scales = keep.tile([P, PAIR], U8, name="first_scales", align_bytes=64)
        h_codes = keep.tile([P, S], U32, name="h_codes", align_bytes=64)
        h_scales = keep.tile([P, S], U8, name="h_scales", align_bytes=64)
        gates = keep.tile([P, S], F32, name="gates")
        routed = [keep.tile([P, T], F32, name="routed%d" % b) for b in range(4)]
        result = {}

        nc.sync.dma_start(offsets[:], offs)
        nc.sync.dma_start(token_words[:], x_words[0].rearrange("p t r -> p (t r)").bitcast(I32))
        for q in range(4):
            nc.sync.dma_start(
                token_scales[32 * q : 32 * q + 32, :].bitcast(I32),
                x_scales[0, 4 * q : 4 * q + 4, :].bitcast(I32).partition_broadcast(8),
            )
        for b in range(4):
            nc.gpsimd.memset(routed[b][:], 0.0)

        on_pe = [sum(1 for step in STEPS if step[:2] == "p%d" % b) for b in range(4)]
        if max(on_pe):
            identity = keep.tile([P, P], F32, name="identity")
            make_identity(nc, identity[:])

        def arena_tile(key, shape, size):
            return arena.tile(shape, F32, name="raw", bufs=RAW)

        def staged(shape, dtype):
            return work.tile(shape, dtype, name="stage", align_bytes=64, bufs=RING)

        w1_raw = {}
        w2_raw = {}
        for load in LOADS:
            kind, e = load[0], int(load[1])
            if kind == "a":
                tile = arena_tile(load, [P, PACK, H], 8192)
                nc.sync.dma_start(tile[:], w1[e].rearrange("(p j) c -> p j c", j=PACK))
                w1_raw[e] = tile
            elif kind == "b" and len(load) == 2:
                tile = arena_tile(load, [P, PACK, N], 8192)
                nc.sync.dma_start(tile[:], w2[e].rearrange("(p j) c -> p j c", j=PACK))
                for half in range(2):
                    w2_raw[e, half] = tile[:, :, half * HALF : (half + 1) * HALF]
            elif kind == "b":
                half = int(load[2])
                tile = arena_tile(load, [P, PACK, HALF], 4096)
                nc.sync.dma_start(
                    tile[:], w2[e].rearrange("(p j) c -> p j c", j=PACK)[:, :, half * HALF : (half + 1) * HALF]
                )
                w2_raw[e, half] = tile[:]
            else:
                cols = slice(0, PAIR) if e == 0 else slice(PAIR, S)
                nc.sync.dma_start(gates[:, cols], gate[:P, cols])

        nc.vector.tensor_copy(slot_words[:], token_words[:].bitcast(U32).indirect(offsets[:]))
        nc.vector.tensor_copy(first_scales[:], token_scales[:].indirect(offsets[:, :16]))
        slot_scales = {0: first_scales[:, :C], 1: first_scales[:, C:]}

        grouped = {}
        turned = {}
        filled = {}
        acc1 = {}
        acc2 = {}
        w2_q = {}
        relu_done = set()
        multiplied = set()
        scattered = [0] * 4

        def group_tile(key):
            if key not in grouped:
                grouped[key] = staged([P, 4 * H], BF16)
                filled[key] = 0
            filled[key] += 1
            return grouped[key]

        def copy(on_vector, dst, src):
            if on_vector:
                nc.vector.tensor_copy(out=dst, in_=src)
            else:
                nc.scalar.copy(out=dst, in_=src)

        def quantise(key):
            codes = work.tile([P, H], U32, name="codes_" + key[1], align_bytes=64)
            scales = work.tile([P, H], U8, name="scales_" + key[1], align_bytes=64)
            nc.vector.quantize_mx(codes[:].bitcast(FP8X4), scales[:], grouped[key][:])
            return codes, scales

        def mx(acc, lhs, lhs_scales, rhs, rhs_scales):
            nc.tensor.matmul_mx(
                out=acc,
                lhsT=lhs.bitcast(FP8X4),
                lhsT_scale=lhs_scales,
                rhs=rhs.bitcast(FP8X4),
                rhs_scale=rhs_scales,
                start=True,
                stop=True,
            )

        def second_products():
            for e, half in list(w2_q):
                if e in relu_done and (e, half) not in multiplied:
                    multiplied.add((e, half))
                    pair, u = divmod(e, 2)
                    if (pair, half) not in acc2:
                        acc2[pair, half] = psum.tile([P, 2, PAIR], F32, name="acc2")
                    codes, scales = w2_q[e, half]
                    slots = slice(e * C, (e + 1) * C)
                    for v in range(2):
                        cols = slice(v * P, (v + 1) * P)
                        mx(
                            acc2[pair, half][:, v, u * C : (u + 1) * C],
                            codes[:, cols],
                            scales[:, cols],
                            h_codes[:, slots],
                            h_scales[:, slots],
                        )

        for step in STEPS:
            kind = step[0]
            on_vector = step[-1] == "v"
            if kind == "a":
                e, half = int(step[1]), int(step[2])
                key = "Ga%d" % e
                tile = group_tile(key)
                src = w1_raw[e][:].rearrange("p j (m t) -> p m j t", t=PACK)
                dst = tile[:].rearrange("p (t m j) -> p m j t", t=PACK, j=PACK)
                if T_SPLIT:
                    ts = slice(half * 2, half * 2 + 2)
                    copy(on_vector, dst[:, :, :, ts], src[:, :, :, ts])
                else:
                    ms = slice(half * 64, (half + 1) * 64)
                    copy(on_vector, dst[:, ms], src[:, ms])
                if filled[key] == 2:
                    codes, scales = quantise(key)
                    acc = psum.tile([P, PACK, C], F32, name="acc1")
                    slots = slice(e * C, (e + 1) * C)
                    for t in range(PACK):
                        cols = slice(t * P, (t + 1) * P)
                        mx(acc[:, t, :], codes[:, cols], scales[:, cols], slot_words[:, slots], slot_scales[e])
                    acc1[e] = acc
            elif kind == "x":
                for b in X_ORDER:
                    result[b] = arena_tile("x", [P, T], 6144)
                    nc.sync.dma_start(result[b][:], xr[b * P : (b + 1) * P, :])
            elif kind == "p":
                b, chunk = int(step[1]), int(step[2])
                assert scattered[b] == 4 and chunk < on_pe[b]
                summed = psum.tile([P, 4, P], F32, name="acc1")
                for i in range(4):
                    part = slice(chunk * 512 + i * P, chunk * 512 + (i + 1) * P)
                    for first, source in ((True, result[b]), (False, routed[b])):
                        nc.tensor.matmul(
                            summed[:, i, :], source[:, part], identity[:], start=first, stop=not first, is_transpose=True
                        )
                turned[b, chunk] = staged([P, 4, P], F32)
                nc.scalar.copy(out=turned[b, chunk][:], in_=summed[:])
            elif kind == "o":
                b, chunk = int(step[1]), int(step[2])
                cols = slice(chunk * 512, (chunk + 1) * 512)
                back = psum.tile([P, 4, P], F32, name="acc1")
                for i in range(4):
                    nc.tensor.transpose(back[:, i, :], turned[b, chunk][:, i, :], identity[:])
                nc.scalar.copy(out=result[b][:, cols], in_=back[:].rearrange("p i t -> p (i t)"))
                nc.sync.dma_start(out[b * P : (b + 1) * P, cols], result[b][:, cols])
            elif kind == "e":
                b = int(step[1])
                assert scattered[b] == 4
                start = on_pe[b] * 512
                cuts = LAST_CUTS if step == [other for other in STEPS if other[0] == "e"][-1] else 1
                for cut in range(cuts if start < T else 0):
                    cols = slice(start + cut * (T - start) // cuts, start + (cut + 1) * (T - start) // cuts)
                    nc.vector.tensor_tensor(result[b][:, cols], result[b][:, cols], routed[b][:, cols], ADD)
                    nc.sync.dma_start(out[b * P : (b + 1) * P, cols], result[b][:, cols])
            elif kind == "s":
                rest = staged([P, S - PAIR], U8)
                nc.vector.tensor_copy(rest[:], token_scales[:].indirect(offsets[:, 16:]))
                for later in range(2, E):
                    slot_scales[later] = rest[:, (later - 2) * C : (later - 1) * C]
            elif kind == "r":
                e = int(step[1])
                hidden = staged([P, C, PACK], BF16)
                nc.scalar.activation(hidden[:], acc1[e][:].rearrange("p t c -> p c t"), RELU)
                slots = slice(e * C, (e + 1) * C)
                nc.vector.quantize_mx(
                    h_codes[:, slots].bitcast(FP8X4), h_scales[:, slots], hidden[:].rearrange("p c t -> p (c t)")
                )
                relu_done.add(e)
                second_products()
            elif kind == "b":
                e, half = int(step[1]), int(step[2])
                pair, u = divmod(e, 2)
                by_half = pair in BY_HALF
                key = "Gb%d%d" % (pair, half if by_half else u)
                part = u if by_half else half
                tile = group_tile(key)
                dst = tile[:, part * 4 * HALF : (part + 1) * 4 * HALF]
                if step[-1] == "g":
                    nc.gpsimd.tensor_scalar(
                        dst.rearrange("p (c j) -> p c j", j=PACK),
                        w2_raw[e, half].rearrange("p j c -> p c j"),
                        1.0,
                        0.0,
                        MULT,
                        ADD,
                    )
                else:
                    copy(
                        on_vector,
                        dst.rearrange("p (c i j) -> p c j i", i=4, j=PACK),
                        w2_raw[e, half].rearrange("p j (c i) -> p c j i", i=4),
                    )
                if filled[key] == 2:
                    codes, scales = quantise(key)
                    for other in range(2):
                        cols = slice(other * HALF, (other + 1) * HALF)
                        owner = (2 * pair + other, half) if by_half else (e, other)
                        w2_q[owner] = codes[:, cols], scales[:, cols]
                    second_products()
            else:
                pair, b = int(step[1]), int(step[2])
                assert (2 * pair, b // 2) in multiplied and (2 * pair + 1, b // 2) in multiplied
                y = staged([P, PAIR], F32)
                window = routed[b][:].indirect(offsets[:, pair * 16 : (pair + 1) * 16])
                sums = acc2[pair, b // 2][:, b % 2, :]
                weights = gates[:, pair * PAIR : (pair + 1) * PAIR]
                if kind == "y":
                    nc.scalar.copy(out=y[:], in_=sums)
                    nc.vector.tensor_tensor(window, y[:], weights, MULT)
                else:
                    nc.vector.tensor_tensor(y[:], sums, weights, MULT)
                    nc.vector.tensor_copy(window, y[:])
                scattered[b] += 1
